import numpy as np
import ml_dtypes


def mxq(x, axis, fmt="e4m3"):
    dtype, down = {"e4m3": (ml_dtypes.float8_e4m3fn, 7), "e5m2": (ml_dtypes.float8_e5m2, 14)}[fmt]
    v = np.moveaxis(np.asarray(x, np.float32).astype(ml_dtypes.bfloat16).astype(np.float64), axis, -1)
    blocks = v.reshape(v.shape[:-1] + (-1, 32))
    amax = np.abs(blocks).max(-1, keepdims=True)
    byte = np.maximum(np.where(amax > 0, np.frexp(amax)[1] - 1 + 127, 0) - down, 1)
    scale = np.exp2(byte - 127.0)
    codes = (blocks / scale).astype(np.float32).astype(dtype).astype(np.float64)
    return np.moveaxis((codes * scale).reshape(v.shape), -1, axis)


WIDE = False


def mx_kscale(k):
    if not WIDE:
        return np.ones(k)
    levels = np.array([10, -10, 5, -5, 0])
    if k % 512:
        return np.exp2(np.random.permutation(np.resize(levels, k // 32))).repeat(32)
    a = np.empty((k // 512, 16))
    for p in range(k // 512):
        a[p, :8] = np.random.permutation(np.resize(levels, 8))
        for g in range(8):
            far = levels[np.abs(levels - a[p, g]) >= 10]
            a[p, g + 8] = far[np.random.randint(len(far))]
    return np.exp2(a.ravel()).repeat(32)


def f64(x):
    return np.asarray(x).astype(np.float64)


def striped8(idx):
    return np.asarray(idx).reshape(8, -1, 16).transpose(0, 2, 1).reshape(128, -1).astype(np.uint16)


def unstriped8(offs):
    return offs.reshape(8, 16, -1).transpose(0, 2, 1).reshape(8, -1).astype(np.int64)


def pick8(x, idx, run):
    r = np.arange(len(x))
    return x[r[:, None], idx[r % (8 * run) // run]]


E2M1 = np.array([0.0, 0.5, 1.0, 1.5, 2.0, 3.0, 4.0, 6.0, -0.0, -0.5, -1.0, -1.5, -2.0, -3.0, -4.0, -6.0])


def pack_weight(w, fmt):
    k, n = w.shape
    w = f64(np.asarray(w, np.float32).astype(ml_dtypes.bfloat16)).reshape(k // 32, 32, n)
    amax = np.abs(w).max(1)
    if fmt == "e4m3":
        byte = np.frexp(amax)[1] - 1 + 127 - 7
    else:
        mant, ex = np.frexp(amax / 6.0)
        byte = np.where(mant > 0.5, ex, ex - 1) + 127
    byte = np.clip(np.where(amax > 0, byte, 1), 1, 254)
    scaled = (w * np.exp2(127.0 - byte)[:, None, :]).reshape(k, n).astype(np.float32)
    by_word = np.ascontiguousarray(scaled.reshape(k // 512, 128, 4, n).transpose(0, 1, 3, 2))
    if fmt == "e4m3":
        words = by_word.astype(ml_dtypes.float8_e4m3fn).view(np.uint8)
    else:
        c = by_word.astype(ml_dtypes.float4_e2m1fn).view(np.uint8) & 0xF
        words = (c[..., 0::2] | (c[..., 1::2] << 4)).reshape(k // 512, 128, 2 * n)
    return np.ascontiguousarray(words), np.ascontiguousarray(byte.astype(np.uint8).reshape(k // 512, 16, n))


def unpack_weight(words, scales, fmt):
    g, _, n = scales.shape
    words = np.ascontiguousarray(words).reshape(g, 128, n, -1)
    if fmt == "e4m3":
        vals = words.view(ml_dtypes.float8_e4m3fn).astype(np.float64)
    else:
        nib = np.empty((g, 128, n, 4), np.uint8)
        nib[..., 0::2] = words & 0xF
        nib[..., 1::2] = words >> 4
        vals = E2M1[nib]
    vals = vals * np.repeat(np.exp2(scales.astype(np.float64) - 127.0), 8, axis=1)[..., None]
    return vals.transpose(0, 1, 3, 2).reshape(g * 512, n)


def sigmoid(v):
    return 1.0 / (1.0 + np.exp(-v))


D, T, I, Q = 512, 1024, 512, 128


def setup_inputs():
    n = np.random.standard_normal
    idx = np.stack([np.random.permutation(T)[:I] for _ in range(8)])
    idx2 = np.stack([np.random.permutation(T)[:I] for _ in range(8)])
    idx3 = np.stack([np.random.permutation(T)[:I] for _ in range(8)])
    fd = mx_kscale(D)
    keysp = pack_weight(n((D, T)) / fd[:, None], "e2m1")
    return {
        "query": (n((D, Q)) * 1.0 / np.sqrt(D) * fd[:, None]).astype(np.float32),
        "keys_words": keysp[0],
        "keys_scales": keysp[1],
        "old": (1.0 * n((Q, T))).astype(np.float32),
        "offs": striped8(idx),
        "offs2": striped8(idx2),
        "offs3": striped8(idx3),
    }


def reference(query, keys_words, keys_scales, old, offs, offs2, offs3):
    idx = unstriped8(offs)
    idx2 = unstriped8(offs2)
    idx3 = unstriped8(offs3)
    keysu = unpack_weight(keys_words, keys_scales, "e2m1")
    queryq = mxq(f64(query), 0, "e4m3")
    a = queryq.T @ keysu
    s = pick8(a, idx, 16) - pick8(a, idx2, 16)
    w = sigmoid(s)
    f1 = np.zeros((Q, T))
    f1[np.arange(Q)[:, None], idx[np.arange(Q) % 128 // 16]] = w
    f2 = f1 + f64(old)
    y = pick8(f2, idx3, 16)
    return y

@@ -1,0 +1,110 @@
+from contextlib import ExitStack
+
+import concourse.mybir as mybir
+
+D, T, I, Q = 512, 1024, 512, 128
+FLOPS = 2 * D * T * Q
+
+F32 = mybir.dt.float32
+BF16 = mybir.dt.bfloat16
+I32 = mybir.dt.int32
+U32 = mybir.dt.uint32
+U16 = mybir.dt.uint16
+U8 = mybir.dt.uint8
+FP8X4 = mybir.dt.float8_e4m3fn_x4
+FP4X4 = mybir.dt.float4_e2m1fn_x4
+ALU = mybir.AluOpType
+ACT = mybir.ActivationFunctionType
+
+P = 128
+PACK = 4
+N_TILE = 256
+HALF = I // 2
+GROUP = 16
+
+
+def tile_attend_difference_lean_through_heads_kernel(tc, query, keys_words, keys_scales, old, offs, offs2, offs3, out):
+    nc = tc.nc
+    with ExitStack() as ctx:
+        sb = ctx.enter_context(tc.tile_pool(name="sb", bufs=1))
+        ps = ctx.enter_context(tc.psum_pool(name="ps", bufs=1))
+
+        q_raw = sb.tile([P, PACK, Q], F32, name="q_raw")
+        q_bf = sb.tile([P, Q, PACK], BF16, name="q_bf", align_bytes=64)
+        q_codes = sb.tile([P, Q], U32, name="q_codes", align_bytes=64)
+        q_scales = sb.tile([P, Q], U8, name="q_scales", align_bytes=64)
+        k_words = sb.tile([P, 2 * T], U8, name="k_words", align_bytes=64)
+        k_scales = sb.tile([P, T], U8, name="k_scales", align_bytes=64)
+        list1 = sb.tile([P, I // GROUP], U16, name="list1")
+        list2 = sb.tile([P, I // GROUP], U16, name="list2")
+        list3 = sb.tile([P, I // GROUP], U16, name="list3")
+        old_sb = sb.tile([P, T], F32, name="old_sb")
+        a = sb.tile([P, T], F32, name="a")
+        f1 = sb.tile([P, T], F32, name="f1")
+        f2 = sb.tile([P, T], F32, name="f2")
+
+        nc.vector.memset(k_scales[:].bitcast(I32), 0)
+        nc.vector.memset(f1[:], 0.0)
+
+        nc.sync.dma_start(out=q_raw[:], in_=query.rearrange("(p j) q -> p j q", j=PACK))
+        nc.sync.dma_start(out=k_words[:], in_=keys_words[0])
+        for quad in range(4):
+            nc.sync.dma_start(
+                out=k_scales[32 * quad : 32 * quad + 4, :].bitcast(I32),
+                in_=keys_scales[0, 4 * quad : 4 * quad + 4, :].bitcast(I32),
+            )
+        nc.sync.dma_start(list2[:], offs2)
+        nc.sync.dma_start(list1[:], offs)
+        nc.sync.dma_start(out=old_sb[:], in_=old)
+        nc.sync.dma_start(list3[:], offs3)
+
+        nc.vector.tensor_copy(
+            out=q_bf[:].rearrange("p (c i) j -> p c j i", i=4),
+            in_=q_raw[:].rearrange("p j (c i) -> p c j i", i=4),
+        )
+        nc.vector.quantize_mx(
+            out=q_codes[:].bitcast(FP8X4),
+            scales=q_scales[:],
+            in_=q_bf[:].rearrange("p q j -> p (q j)"),
+        )
+
+        for n in range(T // N_TILE):
+            cols = slice(n * N_TILE, (n + 1) * N_TILE)
+            acc = ps.tile([Q, N_TILE], F32, name=f"acc{n}")
+            nc.tensor.matmul_mx(
+                out=acc[:],
+                lhsT=q_codes[:].bitcast(FP8X4),
+                lhsT_scale=q_scales[:],
+                rhs=k_words[:, 2 * n * N_TILE : 2 * (n + 1) * N_TILE].bitcast(FP4X4),
+                rhs_scale=k_scales[:, cols],
+                start=True,
+                stop=True,
+            )
+            if n % 2 == 0:
+                nc.vector.tensor_copy(out=a[:, cols], in_=acc[:])
+            else:
+                nc.scalar.copy(out=a[:, cols], in_=acc[:])
+
+        def entries(lst, h):
+            return lst[:, h * HALF // GROUP : (h + 1) * HALF // GROUP]
+
+        second = [sb.tile([P, HALF], F32, name=f"second{h}") for h in range(2)]
+        s = [sb.tile([P, HALF], F32, name=f"s{h}") for h in range(2)]
+        w = [sb.tile([P, HALF], F32, name=f"w{h}") for h in range(2)]
+        y = [sb.tile([P, HALF], F32, name=f"y{h}") for h in range(2)]
+
+        nc.vector.tensor_copy(second[0][:], a[:].indirect(entries(list2, 0)))
+        nc.scalar.activation(second[1][:], a[:].indirect(entries(list2, 1)), ACT.Copy)
+        for h in range(2):
+            nc.vector.tensor_tensor(s[h][:], a[:].indirect(entries(list1, h)), second[h][:], ALU.subtract)
+        for h in range(2):
+            nc.scalar.activation(w[h][:], s[h][:], ACT.Sigmoid)
+        for h in range(2):
+            nc.vector.tensor_copy(f1[:].indirect(entries(list1, h)), w[h][:])
+
+        nc.vector.tensor_tensor(f2[:], f1[:], old_sb[:], ALU.add)
+
+        nc.vector.tensor_copy(y[0][:], f2[:].indirect(entries(list3, 0)))
+        nc.scalar.activation(y[1][:], f2[:].indirect(entries(list3, 1)), ACT.Copy)
+        nc.sync.dma_start(out=out[:, 0:HALF], in_=y[0][:])
+        nc.scalar.dma_start(out=out[:, HALF:I], in_=y[1][:])

@@ -58,6 +58,9 @@ def tile_attend_difference_lean_through_heads_kernel(tc, query, keys_words, keys
         nc.sync.dma_start(out=old_sb[:], in_=old)
         nc.sync.dma_start(list3[:], offs3)
 
+        warm = sb.tile([P, 1], F32, name="warm")
+        nc.scalar.activation(warm[:], q_raw[:, 0, 0:1], ACT.Sigmoid)
+
         nc.vector.tensor_copy(
             out=q_bf[:].rearrange("p (c i) j -> p c j i", i=4),
             in_=q_raw[:].rearrange("p j (c i) -> p c j i", i=4),

@@ -18,9 +18,11 @@ ACT = mybir.ActivationFunctionType
 
 P = 128
 PACK = 4
-N_TILE = 256
+WIDTHS = [256, 256, 256, 128, 128]
 HALF = I // 2
 GROUP = 16
+QV = 64
+LEAD = 128
 
 
 def tile_attend_difference_lean_through_heads_kernel(tc, query, keys_words, keys_scales, old, offs, offs2, offs3, out):
@@ -33,7 +35,7 @@ def tile_attend_difference_lean_through_heads_kernel(tc, query, keys_words, keys
         q_bf = sb.tile([P, Q, PACK], BF16, name="q_bf", align_bytes=64)
         q_codes = sb.tile([P, Q], U32, name="q_codes", align_bytes=64)
         q_scales = sb.tile([P, Q], U8, name="q_scales", align_bytes=64)
-        k_words = sb.tile([P, 2 * T], U8, name="k_words", align_bytes=64)
+        k_words = [sb.tile([P, T], U8, name=f"k_words{h}", align_bytes=64) for h in range(2)]
         k_scales = sb.tile([P, T], U8, name="k_scales", align_bytes=64)
         list1 = sb.tile([P, I // GROUP], U16, name="list1")
         list2 = sb.tile([P, I // GROUP], U16, name="list2")
@@ -47,23 +49,30 @@ def tile_attend_difference_lean_through_heads_kernel(tc, query, keys_words, keys
         nc.vector.memset(f1[:], 0.0)
 
         nc.sync.dma_start(out=q_raw[:], in_=query.rearrange("(p j) q -> p j q", j=PACK))
-        nc.sync.dma_start(out=k_words[:], in_=keys_words[0])
+        nc.sync.dma_start(out=k_words[0][:], in_=keys_words[0, :, 0:T])
         for quad in range(4):
             nc.sync.dma_start(
                 out=k_scales[32 * quad : 32 * quad + 4, :].bitcast(I32),
                 in_=keys_scales[0, 4 * quad : 4 * quad + 4, :].bitcast(I32),
             )
+        nc.sync.dma_start(out=k_words[1][:], in_=keys_words[0, :, T : 2 * T])
         nc.sync.dma_start(list2[:], offs2)
         nc.sync.dma_start(list1[:], offs)
         nc.sync.dma_start(out=old_sb[:], in_=old)
         nc.sync.dma_start(list3[:], offs3)
 
         warm = sb.tile([P, 1], F32, name="warm")
-        nc.scalar.activation(warm[:], q_raw[:, 0, 0:1], ACT.Sigmoid)
+        warm_out = sb.tile([P, 1], F32, name="warm_out")
+        nc.gpsimd.memset(warm[:], 0.0)
+        nc.scalar.activation(warm_out[:], warm[:], ACT.Sigmoid)
 
         nc.vector.tensor_copy(
-            out=q_bf[:].rearrange("p (c i) j -> p c j i", i=4),
-            in_=q_raw[:].rearrange("p j (c i) -> p c j i", i=4),
+            out=q_bf[:, 0:QV, :].rearrange("p (c i) j -> p c j i", i=4),
+            in_=q_raw[:, :, 0:QV].rearrange("p j (c i) -> p c j i", i=4),
+        )
+        nc.scalar.copy(
+            out=q_bf[:, QV:Q, :].rearrange("p (c i) j -> p c j i", i=4),
+            in_=q_raw[:, :, QV:Q].rearrange("p j (c i) -> p c j i", i=4),
         )
         nc.vector.quantize_mx(
             out=q_codes[:].bitcast(FP8X4),
@@ -71,43 +80,46 @@ def tile_attend_difference_lean_through_heads_kernel(tc, query, keys_words, keys
             in_=q_bf[:].rearrange("p q j -> p (q j)"),
         )
 
-        for n in range(T // N_TILE):
-            cols = slice(n * N_TILE, (n + 1) * N_TILE)
-            acc = ps.tile([Q, N_TILE], F32, name=f"acc{n}")
+        n0 = 0
+        for n, width in enumerate(WIDTHS):
+            cols = slice(n0, n0 + width)
+            acc = ps.tile([Q, width], F32, name=f"acc{n}")
             nc.tensor.matmul_mx(
                 out=acc[:],
                 lhsT=q_codes[:].bitcast(FP8X4),
                 lhsT_scale=q_scales[:],
-                rhs=k_words[:, 2 * n * N_TILE : 2 * (n + 1) * N_TILE].bitcast(FP4X4),
+                rhs=k_words[n0 // (T // 2)][:, 2 * (n0 % (T // 2)) : 2 * (n0 % (T // 2) + width)].bitcast(FP4X4),
                 rhs_scale=k_scales[:, cols],
                 start=True,
                 stop=True,
             )
-            if n % 2 == 0:
+            if n % 2 == 1:
                 nc.vector.tensor_copy(out=a[:, cols], in_=acc[:])
             else:
                 nc.scalar.copy(out=a[:, cols], in_=acc[:])
+            n0 = n0 + width
 
-        def entries(lst, h):
-            return lst[:, h * HALF // GROUP : (h + 1) * HALF // GROUP]
+        def entries(lst, lo, hi):
+            return lst[:, lo // GROUP : hi // GROUP]
 
-        second = [sb.tile([P, HALF], F32, name=f"second{h}") for h in range(2)]
-        s = [sb.tile([P, HALF], F32, name=f"s{h}") for h in range(2)]
-        w = [sb.tile([P, HALF], F32, name=f"w{h}") for h in range(2)]
+        halves = [(0, HALF), (HALF, I)]
+        first = sb.tile([P, I], F32, name="first")
+        second = sb.tile([P, I], F32, name="second")
+        s = sb.tile([P, I], F32, name="s")
+        w = sb.tile([P, I], F32, name="w")
         y = [sb.tile([P, HALF], F32, name=f"y{h}") for h in range(2)]
 
-        nc.vector.tensor_copy(second[0][:], a[:].indirect(entries(list2, 0)))
-        nc.scalar.activation(second[1][:], a[:].indirect(entries(list2, 1)), ACT.Copy)
-        for h in range(2):
-            nc.vector.tensor_tensor(s[h][:], a[:].indirect(entries(list1, h)), second[h][:], ALU.subtract)
-        for h in range(2):
-            nc.scalar.activation(w[h][:], s[h][:], ACT.Sigmoid)
-        for h in range(2):
-            nc.vector.tensor_copy(f1[:].indirect(entries(list1, h)), w[h][:])
-
+        for lo, hi in halves:
+            nc.vector.tensor_copy(first[:, lo:hi], a[:].indirect(entries(list1, lo, hi)))
+            nc.scalar.activation(second[:, lo:hi], a[:].indirect(entries(list2, lo, hi)), ACT.Copy)
+        for lo, hi in halves:
+            nc.vector.tensor_tensor(s[:, lo:hi], first[:, lo:hi], second[:, lo:hi], ALU.subtract)
+        for lo, hi in [(0, LEAD), (LEAD, I)]:
+            nc.scalar.activation(w[:, lo:hi], s[:, lo:hi], ACT.Sigmoid)
+            nc.vector.tensor_copy(f1[:].indirect(entries(list1, lo, hi)), w[:, lo:hi])
         nc.vector.tensor_tensor(f2[:], f1[:], old_sb[:], ALU.add)
 
-        nc.vector.tensor_copy(y[0][:], f2[:].indirect(entries(list3, 0)))
-        nc.scalar.activation(y[1][:], f2[:].indirect(entries(list3, 1)), ACT.Copy)
+        nc.vector.tensor_copy(y[0][:], f2[:].indirect(entries(list3, 0, HALF)))
+        nc.scalar.activation(y[1][:], f2[:].indirect(entries(list3, HALF, I)), ACT.Copy)
         nc.sync.dma_start(out=out[:, 0:HALF], in_=y[0][:])
         nc.scalar.dma_start(out=out[:, HALF:I], in_=y[1][:])

@@ -1,6 +1,7 @@
 from contextlib import ExitStack
 
 import concourse.mybir as mybir
+from concourse.masks import make_identity
 
 D, T, I, Q = 512, 1024, 512, 128
 FLOPS = 2 * D * T * Q
@@ -23,6 +24,8 @@ HALF = I // 2
 GROUP = 16
 QV = 64
 LEAD = 128
+BANK = 512
+ADD_V = 768
 
 
 def tile_attend_difference_lean_through_heads_kernel(tc, query, keys_words, keys_scales, old, offs, offs2, offs3, out):
@@ -46,6 +49,9 @@ def tile_attend_difference_lean_through_heads_kernel(tc, query, keys_words, keys
         f2 = sb.tile([P, T], F32, name="f2")
 
         nc.vector.memset(k_scales[:].bitcast(I32), 0)
+        ident = sb.tile([P, P], F32, name="ident")
+        nc.vector.memset(ident[:], 0.0)
+        make_identity(nc, ident[:], nomemset=True)
         nc.vector.memset(f1[:], 0.0)
 
         nc.sync.dma_start(out=q_raw[:], in_=query.rearrange("(p j) q -> p j q", j=PACK))
@@ -83,7 +89,7 @@ def tile_attend_difference_lean_through_heads_kernel(tc, query, keys_words, keys
         n0 = 0
         for n, width in enumerate(WIDTHS):
             cols = slice(n0, n0 + width)
-            acc = ps.tile([Q, width], F32, name=f"acc{n}")
+            acc = ps.tile([Q, width], F32, name=f"acc{n}", tag=f"bank{n}")
             nc.tensor.matmul_mx(
                 out=acc[:],
                 lhsT=q_codes[:].bitcast(FP8X4),
@@ -105,19 +111,34 @@ def tile_attend_difference_lean_through_heads_kernel(tc, query, keys_words, keys
         halves = [(0, HALF), (HALF, I)]
         first = sb.tile([P, I], F32, name="first")
         second = sb.tile([P, I], F32, name="second")
-        s = sb.tile([P, I], F32, name="s")
+        s = sb.tile([P, I], F32, name="s", tag="shared")
         w = sb.tile([P, I], F32, name="w")
         y = [sb.tile([P, HALF], F32, name=f"y{h}") for h in range(2)]
 
         for lo, hi in halves:
             nc.vector.tensor_copy(first[:, lo:hi], a[:].indirect(entries(list1, lo, hi)))
             nc.scalar.activation(second[:, lo:hi], a[:].indirect(entries(list2, lo, hi)), ACT.Copy)
-        for lo, hi in halves:
+        for lo, hi in [(0, LEAD), (LEAD, I)]:
             nc.vector.tensor_tensor(s[:, lo:hi], first[:, lo:hi], second[:, lo:hi], ALU.subtract)
         for lo, hi in [(0, LEAD), (LEAD, I)]:
             nc.scalar.activation(w[:, lo:hi], s[:, lo:hi], ACT.Sigmoid)
             nc.vector.tensor_copy(f1[:].indirect(entries(list1, lo, hi)), w[:, lo:hi])
-        nc.vector.tensor_tensor(f2[:], f1[:], old_sb[:], ALU.add)
+        spans = [(0, BANK), (BANK, ADD_V)]
+        turned = []
+        for n, (lo, hi) in enumerate(spans):
+            bank = ps.tile([P, hi - lo], F32, name=f"turned{n}", tag=f"bank{n}")
+            for c in range(lo, hi, P):
+                nc.tensor.transpose(bank[:, c - lo : c - lo + P], old_sb[:, c : c + P], ident[:])
+            turned.append(bank)
+        old_t = sb.tile([P, ADD_V], F32, name="old_t", tag="shared")
+        for n, (lo, hi) in enumerate(spans):
+            nc.scalar.copy(out=old_t[:, lo:hi], in_=turned[n][:])
+        for n, (lo, hi) in enumerate(spans):
+            bank = ps.tile([P, hi - lo], F32, name=f"old_ps{n}")
+            for c in range(lo, hi, P):
+                nc.tensor.transpose(bank[:, c - lo : c - lo + P], old_t[:, c : c + P], ident[:])
+            nc.vector.tensor_tensor(f2[:, lo:hi], f1[:, lo:hi], bank[:], ALU.add)
+        nc.gpsimd.tensor_tensor(f2[:, ADD_V:T], f1[:, ADD_V:T], old_sb[:, ADD_V:T], ALU.add)
 
         nc.vector.tensor_copy(y[0][:], f2[:].indirect(entries(list3, 0, HALF)))
         nc.scalar.activation(y[1][:], f2[:].indirect(entries(list3, HALF, I)), ACT.Copy)

@@ -22,10 +22,10 @@ PACK = 4
 WIDTHS = [256, 256, 256, 128, 128]
 HALF = I // 2
 GROUP = 16
-QV = 64
+QV = 88
 LEAD = 128
 BANK = 512
-ADD_V = 768
+ADD_V = 640
 
 
 def tile_attend_difference_lean_through_heads_kernel(tc, query, keys_words, keys_scales, old, offs, offs2, offs3, out):

from contextlib import ExitStack

import concourse.mybir as mybir
from concourse.masks import make_identity

D, T, I, Q = 512, 1024, 512, 128
FLOPS = 2 * D * T * Q

F32 = mybir.dt.float32
BF16 = mybir.dt.bfloat16
I32 = mybir.dt.int32
U32 = mybir.dt.uint32
U16 = mybir.dt.uint16
U8 = mybir.dt.uint8
FP8X4 = mybir.dt.float8_e4m3fn_x4
FP4X4 = mybir.dt.float4_e2m1fn_x4
ALU = mybir.AluOpType
ACT = mybir.ActivationFunctionType

P = 128
PACK = 4
WIDTHS = [256, 256, 256, 128, 128]
HALF = I // 2
GROUP = 16
QV = 88
LEAD = 128
BANK = 512
ADD_V = 640


def tile_attend_difference_lean_through_heads_kernel(tc, query, keys_words, keys_scales, old, offs, offs2, offs3, out):
    nc = tc.nc
    with ExitStack() as ctx:
        sb = ctx.enter_context(tc.tile_pool(name="sb", bufs=1))
        ps = ctx.enter_context(tc.psum_pool(name="ps", bufs=1))

        q_raw = sb.tile([P, PACK, Q], F32, name="q_raw")
        q_bf = sb.tile([P, Q, PACK], BF16, name="q_bf", align_bytes=64)
        q_codes = sb.tile([P, Q], U32, name="q_codes", align_bytes=64)
        q_scales = sb.tile([P, Q], U8, name="q_scales", align_bytes=64)
        k_words = [sb.tile([P, T], U8, name=f"k_words{h}", align_bytes=64) for h in range(2)]
        k_scales = sb.tile([P, T], U8, name="k_scales", align_bytes=64)
        list1 = sb.tile([P, I // GROUP], U16, name="list1")
        list2 = sb.tile([P, I // GROUP], U16, name="list2")
        list3 = sb.tile([P, I // GROUP], U16, name="list3")
        old_sb = sb.tile([P, T], F32, name="old_sb")
        a = sb.tile([P, T], F32, name="a")
        f1 = sb.tile([P, T], F32, name="f1")
        f2 = sb.tile([P, T], F32, name="f2")

        nc.vector.memset(k_scales[:].bitcast(I32), 0)
        ident = sb.tile([P, P], F32, name="ident")
        nc.vector.memset(ident[:], 0.0)
        make_identity(nc, ident[:], nomemset=True)
        nc.vector.memset(f1[:], 0.0)

        nc.sync.dma_start(out=q_raw[:], in_=query.rearrange("(p j) q -> p j q", j=PACK))
        nc.sync.dma_start(out=k_words[0][:], in_=keys_words[0, :, 0:T])
        for quad in range(4):
            nc.sync.dma_start(
                out=k_scales[32 * quad : 32 * quad + 4, :].bitcast(I32),
                in_=keys_scales[0, 4 * quad : 4 * quad + 4, :].bitcast(I32),
            )
        nc.sync.dma_start(out=k_words[1][:], in_=keys_words[0, :, T : 2 * T])
        nc.sync.dma_start(list2[:], offs2)
        nc.sync.dma_start(list1[:], offs)
        nc.sync.dma_start(out=old_sb[:], in_=old)
        nc.sync.dma_start(list3[:], offs3)

        warm = sb.tile([P, 1], F32, name="warm")
        warm_out = sb.tile([P, 1], F32, name="warm_out")
        nc.gpsimd.memset(warm[:], 0.0)
        nc.scalar.activation(warm_out[:], warm[:], ACT.Sigmoid)

        nc.vector.tensor_copy(
            out=q_bf[:, 0:QV, :].rearrange("p (c i) j -> p c j i", i=4),
            in_=q_raw[:, :, 0:QV].rearrange("p j (c i) -> p c j i", i=4),
        )
        nc.scalar.copy(
            out=q_bf[:, QV:Q, :].rearrange("p (c i) j -> p c j i", i=4),
            in_=q_raw[:, :, QV:Q].rearrange("p j (c i) -> p c j i", i=4),
        )
        nc.vector.quantize_mx(
            out=q_codes[:].bitcast(FP8X4),
            scales=q_scales[:],
            in_=q_bf[:].rearrange("p q j -> p (q j)"),
        )

        n0 = 0
        for n, width in enumerate(WIDTHS):
            cols = slice(n0, n0 + width)
            acc = ps.tile([Q, width], F32, name=f"acc{n}", tag=f"bank{n}")
            nc.tensor.matmul_mx(
                out=acc[:],
                lhsT=q_codes[:].bitcast(FP8X4),
                lhsT_scale=q_scales[:],
                rhs=k_words[n0 // (T // 2)][:, 2 * (n0 % (T // 2)) : 2 * (n0 % (T // 2) + width)].bitcast(FP4X4),
                rhs_scale=k_scales[:, cols],
                start=True,
                stop=True,
            )
            if n % 2 == 1:
                nc.vector.tensor_copy(out=a[:, cols], in_=acc[:])
            else:
                nc.scalar.copy(out=a[:, cols], in_=acc[:])
            n0 = n0 + width

        def entries(lst, lo, hi):
            return lst[:, lo // GROUP : hi // GROUP]

        halves = [(0, HALF), (HALF, I)]
        first = sb.tile([P, I], F32, name="first")
        second = sb.tile([P, I], F32, name="second")
        s = sb.tile([P, I], F32, name="s", tag="shared")
        w = sb.tile([P, I], F32, name="w")
        y = [sb.tile([P, HALF], F32, name=f"y{h}") for h in range(2)]

        for lo, hi in halves:
            nc.vector.tensor_copy(first[:, lo:hi], a[:].indirect(entries(list1, lo, hi)))
            nc.scalar.activation(second[:, lo:hi], a[:].indirect(entries(list2, lo, hi)), ACT.Copy)
        for lo, hi in [(0, LEAD), (LEAD, I)]:
            nc.vector.tensor_tensor(s[:, lo:hi], first[:, lo:hi], second[:, lo:hi], ALU.subtract)
        for lo, hi in [(0, LEAD), (LEAD, I)]:
            nc.scalar.activation(w[:, lo:hi], s[:, lo:hi], ACT.Sigmoid)
            nc.vector.tensor_copy(f1[:].indirect(entries(list1, lo, hi)), w[:, lo:hi])
        spans = [(0, BANK), (BANK, ADD_V)]
        turned = []
        for n, (lo, hi) in enumerate(spans):
            bank = ps.tile([P, hi - lo], F32, name=f"turned{n}", tag=f"bank{n}")
            for c in range(lo, hi, P):
                nc.tensor.transpose(bank[:, c - lo : c - lo + P], old_sb[:, c : c + P], ident[:])
            turned.append(bank)
        old_t = sb.tile([P, ADD_V], F32, name="old_t", tag="shared")
        for n, (lo, hi) in enumerate(spans):
            nc.scalar.copy(out=old_t[:, lo:hi], in_=turned[n][:])
        for n, (lo, hi) in enumerate(spans):
            bank = ps.tile([P, hi - lo], F32, name=f"old_ps{n}")
            for c in range(lo, hi, P):
                nc.tensor.transpose(bank[:, c - lo : c - lo + P], old_t[:, c : c + P], ident[:])
            nc.vector.tensor_tensor(f2[:, lo:hi], f1[:, lo:hi], bank[:], ALU.add)
        nc.gpsimd.tensor_tensor(f2[:, ADD_V:T], f1[:, ADD_V:T], old_sb[:, ADD_V:T], ALU.add)

        nc.vector.tensor_copy(y[0][:], f2[:].indirect(entries(list3, 0, HALF)))
        nc.scalar.activation(y[1][:], f2[:].indirect(entries(list3, HALF, I)), ACT.Copy)
        nc.sync.dma_start(out=out[:, 0:HALF], in_=y[0][:])
        nc.scalar.dma_start(out=out[:, HALF:I], in_=y[1][:])
